import numpy as np
import ml_dtypes


def mxq(x, axis, fmt="e4m3"):
    dtype, down = {"e4m3": (ml_dtypes.float8_e4m3fn, 7), "e5m2": (ml_dtypes.float8_e5m2, 14)}[fmt]
    v = np.moveaxis(np.asarray(x, np.float32).astype(ml_dtypes.bfloat16).astype(np.float64), axis, -1)
    blocks = v.reshape(v.shape[:-1] + (-1, 32))
    amax = np.abs(blocks).max(-1, keepdims=True)
    byte = np.maximum(np.where(amax > 0, np.frexp(amax)[1] - 1 + 127, 0) - down, 1)
    scale = np.exp2(byte - 127.0)
    codes = (blocks / scale).astype(np.float32).astype(dtype).astype(np.float64)
    return np.moveaxis((codes * scale).reshape(v.shape), -1, axis)


WIDE = False


def mx_kscale(k):
    if not WIDE:
        return np.ones(k)
    levels = np.array([10, -10, 5, -5, 0])
    if k % 512:
        return np.exp2(np.random.permutation(np.resize(levels, k // 32))).repeat(32)
    a = np.empty((k // 512, 16))
    for p in range(k // 512):
        a[p, :8] = np.random.permutation(np.resize(levels, 8))
        for g in range(8):
            far = levels[np.abs(levels - a[p, g]) >= 10]
            a[p, g + 8] = far[np.random.randint(len(far))]
    return np.exp2(a.ravel()).repeat(32)


def f64(x):
    return np.asarray(x).astype(np.float64)


def striped(idx):
    return np.tile(idx.reshape(-1, 16).T, (8, 1)).astype(np.uint16)


def unstriped(offs):
    return offs[:16].T.reshape(-1).astype(np.int64)


def pack_weight(w):
    k, n = w.shape
    w = f64(np.asarray(w, np.float32).astype(ml_dtypes.bfloat16)).reshape(k // 32, 32, n)
    amax = np.abs(w).max(1)
    byte = np.clip(np.where(amax > 0, np.frexp(amax)[1] - 1 + 127 - 7, 1), 1, 254)
    scaled = (w * np.exp2(127.0 - byte)[:, None, :]).reshape(k, n).astype(np.float32)
    words = np.ascontiguousarray(scaled.reshape(k // 512, 128, 4, n).transpose(0, 1, 3, 2)).astype(ml_dtypes.float8_e4m3fn).view(np.uint8)
    return words, np.ascontiguousarray(byte.astype(np.uint8).reshape(k // 512, 16, n))


def unpack_weight(words, scales):
    g, p, n, _ = words.shape
    vals = np.ascontiguousarray(words).view(ml_dtypes.float8_e4m3fn).astype(np.float64) * np.repeat(np.exp2(scales.astype(np.float64) - 127.0), 8, axis=1)[..., None]
    return vals.transpose(0, 1, 3, 2).reshape(g * 512, n)


K, T, S, D, N = 512, 4096, 1024, 4, 128


def setup_inputs():
    n = np.random.standard_normal
    s = mx_kscale(K)[:, None]
    packed_xT = pack_weight(n((K, T)) * s)
    return {
        "x_words": packed_xT[0],
        "x_scales": packed_xT[1],
        "w1": (n((K, N)) / np.sqrt(K) / s).astype(np.float32),
        "offs": striped(np.random.permutation(T)[:S]),
    }


def reference(x_words, x_scales, w1, offs):
    xq = unpack_weight(x_words, x_scales)[:, unstriped(offs)]
    y = mxq(f64(w1), 0, "e4m3").T @ xq
    mg = y.reshape(len(y), -1, D).mean(axis=2)
    mt = mg.reshape(len(mg), -1, D).mean(axis=2)
    d2 = (mg - np.repeat(mt, D, axis=1)) ** 2
    vt = d2.reshape(len(d2), -1, D).mean(axis=2) + 0.05
    d1 = (y - np.repeat(mg, D, axis=1)) ** 2
    vg = d1.reshape(len(d1), -1, D).mean(axis=2) + 0.1
    shr = np.repeat(vt, D, axis=1) / (np.repeat(vt, D, axis=1) + 0.25 * vg)
    return np.repeat(mt, D, axis=1) + shr * (mg - np.repeat(mt, D, axis=1))

@@ -1,0 +1,133 @@
+from contextlib import ExitStack
+
+import concourse.mybir as mybir
+
+K, T, S, D, M = 512, 4096, 1024, 4, 128
+FLOPS = 2 * K * M * S
+
+F32 = mybir.dt.float32
+BF16 = mybir.dt.bfloat16
+I32 = mybir.dt.int32
+U32 = mybir.dt.uint32
+U16 = mybir.dt.uint16
+U8 = mybir.dt.uint8
+FP8X4 = mybir.dt.float8_e4m3fn_x4
+ALU = mybir.AluOpType
+ACT = mybir.ActivationFunctionType
+AXIS_X = mybir.AxisListType.X
+
+P = 128
+HALVES = 2
+HS = S // HALVES
+HV = HS // D
+HW = HV // D
+BANKS = 2
+BS = HS // BANKS
+BV = HV // BANKS
+LAG = 2
+
+
+def tile_picked_yhbays_mean_p_kernel(tc, x_words, x_scales, w1, offs, out):
+    nc = tc.nc
+    with ExitStack() as ctx:
+        sb = ctx.enter_context(tc.tile_pool(name="sb", bufs=1))
+        shared = ctx.enter_context(tc.tile_pool(name="shared", bufs=1))
+        ps = ctx.enter_context(tc.psum_pool(name="ps", bufs=1))
+
+        offsets = sb.tile([P, S // 16], U16, name="offsets")
+        words = sb.tile([P, T], U32, name="words", align_bytes=64)
+        scales = shared.tile([P, T], U8, name="scales", align_bytes=64, offset=0)
+        w_raw = sb.tile([P, 4, M], F32, name="w_raw", align_bytes=64)
+
+        nc.vector.memset(scales[:].bitcast(I32), 0)
+        nc.sync.dma_start(offsets[:], offs)
+        nc.scalar.dma_start(words[:].bitcast(I32), x_words[0].rearrange("p n t -> p (n t)").bitcast(I32))
+        nc.sync.dma_start(w_raw[:], w1.rearrange("(p j) m -> p j m", j=4))
+        for q in range(4):
+            nc.sync.dma_start(scales[32 * q : 32 * q + 4, :].bitcast(I32), x_scales[0, 4 * q : 4 * q + 4, :].bitcast(I32))
+
+        one = sb.tile([P, 1], F32, name="one")
+        nc.gpsimd.memset(one[:], 1.0)
+        warm = sb.tile([P, 1], F32, name="warm")
+        nc.scalar.activation(warm[:], one[:], ACT.Abs_reciprocal_sqrt)
+
+        w_bf = shared.tile([P, M, 4], BF16, name="w_bf", align_bytes=64, offset=T)
+        nc.scalar.copy(w_bf[:], w_raw[:].rearrange("p j m -> p m j"))
+        w_codes = sb.tile([P, M], U32, name="w_codes", align_bytes=64)
+        w_scales = sb.tile([P, M], U8, name="w_scales", align_bytes=64)
+
+        g_scales = sb.tile([P, S], U8, name="g_scales", align_bytes=64)
+        nc.vector.tensor_copy(g_scales[:], scales[:].indirect(offsets[:]))
+        plane = g_scales
+
+        nc.vector.quantize_mx(out=w_codes[:].bitcast(FP8X4), scales=w_scales[:], in_=w_bf[:].rearrange("p m j -> p (m j)"))
+
+        g_words = shared.tile([P, S], U32, name="g_words", align_bytes=64, offset=T // 4)
+        ys = {}
+        for h in range(HALVES):
+            nc.vector.tensor_copy(g_words[:, h * HS : (h + 1) * HS], words[:].indirect(offsets[:, h * HS // 16 : (h + 1) * HS // 16]))
+            for b in range(BANKS):
+                cols = slice(h * HS + b * BS, h * HS + (b + 1) * BS)
+                y = ps.tile([P, BS], F32, name=f"y{h}{b}")
+                nc.tensor.matmul_mx(out=y[:], lhsT=w_codes[:].bitcast(FP8X4), lhsT_scale=w_scales[:],
+                                    rhs=g_words[:, cols].bitcast(FP8X4), rhs_scale=plane[:, cols],
+                                    start=True, stop=True)
+                ys[h, b] = y[:].rearrange("p (v d) -> p d v", d=D)
+
+        def steps(h):
+            def f32(name, *shape):
+                return sb.tile([P, *shape], F32, name=f"{name}{h}", align_bytes=64)
+
+            def per_state(t):
+                return t[:].unsqueeze(2).to_broadcast([P, HW, D])
+
+            def by_state(t):
+                return t[:].rearrange("p (w d) -> p w d", d=D)
+
+            late = [f32(f"late{b}", 2, BV) for b in range(BANKS)]
+            psum2 = f32("psum2", 2, HV)
+            pdiff = f32("pdiff", 2, HV)
+            pdiff2 = f32("pdiff2", 2, HV)
+            dsum, cross, cross2, q1, dev, within, dev2, den, root, inv, ta, tb, numer, res = [
+                f32(n, HV) for n in "dsum cross cross2 q1 dev within dev2 den root inv ta tb numer res".split()]
+            ssum = f32("ssum", HW)
+            between = f32("between", HW)
+            tt, stt, act = nc.vector.tensor_tensor, nc.vector.scalar_tensor_tensor, nc.scalar.activation
+
+            def bank(b):
+                return slice(b * BV, (b + 1) * BV)
+
+            work = []
+            for b in range(BANKS):
+                work.append(lambda b=b: nc.scalar.copy(late[b][:], ys[h, b][:, 2:4, :]))
+                work.append(lambda b=b: tt(psum2[:, :, bank(b)], ys[h, b][:, 0:2, :], late[b][:], ALU.add))
+            work.append(lambda: tt(dsum[:], psum2[:, 0, :], psum2[:, 1, :], ALU.add))
+            for b in range(BANKS):
+                work.append(lambda b=b: tt(pdiff[:, :, bank(b)], ys[h, b][:, 0:2, :], late[b][:], ALU.subtract))
+            work.extend([
+                lambda: nc.vector.tensor_reduce(ssum[:], by_state(dsum), AXIS_X, ALU.add),
+                lambda: tt(cross[:], psum2[:, 0, :], psum2[:, 1, :], ALU.subtract),
+                lambda: act(pdiff2[:], pdiff[:], ACT.Square, scale=0.125),
+                lambda: stt(by_state(dev), per_state(ssum), -0.25, by_state(dsum), ALU.mult, ALU.add),
+                lambda: act(dev2[:], dev[:], ACT.Square, scale=0.125),
+                lambda: act(cross2[:], cross[:], ACT.Square, scale=0.125),
+                lambda: tt(q1[:], pdiff2[:, 0, :], pdiff2[:, 1, :], ALU.add),
+                lambda: nc.vector.tensor_reduce(between[:], by_state(dev2), AXIS_X, ALU.add),
+                lambda: stt(within[:], q1[:], 2.0, cross2[:], ALU.mult, ALU.add),
+                lambda: stt(by_state(den), per_state(between), 0.075, by_state(within), ALU.add, ALU.add),
+                lambda: act(root[:], den[:], ACT.Abs_reciprocal_sqrt),
+                lambda: stt(by_state(ta), by_state(within), 0.025, per_state(ssum), ALU.add, ALU.mult),
+                lambda: stt(by_state(tb), per_state(between), 0.05, by_state(dsum), ALU.add, ALU.mult),
+                lambda: act(inv[:], root[:], ACT.Square, scale=0.25),
+                lambda: stt(numer[:], tb[:], 4.0, ta[:], ALU.mult, ALU.add),
+                lambda: tt(res[:], numer[:], inv[:], ALU.mult),
+                lambda: nc.sync.dma_start(out[:, h * HV : (h + 1) * HV], res[:]),
+            ])
+            return work
+
+        first, second = steps(0), steps(1)
+        for i in range(len(first) + LAG):
+            if i >= LAG:
+                second[i - LAG]()
+            if i < len(first):
+                first[i]()

@@ -41,13 +41,12 @@ def tile_picked_yhbays_mean_p_kernel(tc, x_words, x_scales, w1, offs, out):
 
         nc.vector.memset(scales[:].bitcast(I32), 0)
         nc.sync.dma_start(offsets[:], offs)
-        nc.scalar.dma_start(words[:].bitcast(I32), x_words[0].rearrange("p n t -> p (n t)").bitcast(I32))
-        nc.sync.dma_start(w_raw[:], w1.rearrange("(p j) m -> p j m", j=4))
-        for q in range(4):
-            nc.sync.dma_start(scales[32 * q : 32 * q + 4, :].bitcast(I32), x_scales[0, 4 * q : 4 * q + 4, :].bitcast(I32))
+        nc.scalar.dma_start(w_raw[:], w1.rearrange("(p j) m -> p j m", j=4))
+        nc.scalar.dma_start(words[:].bitcast(I32), x_words[0].rearrange("p n t -> p (n t)").bitcast(I32), max_dma_last_dim=4096)
+        nc.sync.dma_start(scales[0:P:8, :].bitcast(I32), x_scales[0].bitcast(I32))
 
         one = sb.tile([P, 1], F32, name="one")
-        nc.gpsimd.memset(one[:], 1.0)
+        nc.vector.memset(one[:], 1.0)
         warm = sb.tile([P, 1], F32, name="warm")
         nc.scalar.activation(warm[:], one[:], ACT.Abs_reciprocal_sqrt)
 
@@ -57,8 +56,13 @@ def tile_picked_yhbays_mean_p_kernel(tc, x_words, x_scales, w1, offs, out):
         w_scales = sb.tile([P, M], U8, name="w_scales", align_bytes=64)
 
         g_scales = sb.tile([P, S], U8, name="g_scales", align_bytes=64)
-        nc.vector.tensor_copy(g_scales[:], scales[:].indirect(offsets[:]))
-        plane = g_scales
+        plane = sb.tile([P, S], U8, name="plane", align_bytes=64)
+        nc.vector.memset(plane[:].bitcast(I32), 0)
+        for h in range(1):
+            cols = slice(h * S // 1, (h + 1) * S // 1)
+            nc.vector.tensor_copy(g_scales[:, cols], scales[:].indirect(offsets[:, h * S // 1 // 16 : (h + 1) * S // 1 // 16]))
+            for q in range(4):
+                nc.sync.dma_start(plane[32 * q : 32 * q + 4, cols].bitcast(I32), g_scales[32 * q : 32 * q + 32 : 8, cols].bitcast(I32))
 
         nc.vector.quantize_mx(out=w_codes[:].bitcast(FP8X4), scales=w_scales[:], in_=w_bf[:].rearrange("p m j -> p (m j)"))
 

@@ -39,11 +39,11 @@ def tile_picked_yhbays_mean_p_kernel(tc, x_words, x_scales, w1, offs, out):
         scales = shared.tile([P, T], U8, name="scales", align_bytes=64, offset=0)
         w_raw = sb.tile([P, 4, M], F32, name="w_raw", align_bytes=64)
 
-        nc.vector.memset(scales[:].bitcast(I32), 0)
+        nc.vector.memset(scales[0:112, :].bitcast(I32), 0)
+        nc.sync.dma_start(scales[112:P, :].bitcast(I32), x_scales[0].bitcast(I32))
         nc.sync.dma_start(offsets[:], offs)
         nc.scalar.dma_start(w_raw[:], w1.rearrange("(p j) m -> p j m", j=4))
         nc.scalar.dma_start(words[:].bitcast(I32), x_words[0].rearrange("p n t -> p (n t)").bitcast(I32), max_dma_last_dim=4096)
-        nc.sync.dma_start(scales[0:P:8, :].bitcast(I32), x_scales[0].bitcast(I32))
 
         one = sb.tile([P, 1], F32, name="one")
         nc.vector.memset(one[:], 1.0)
@@ -62,7 +62,7 @@ def tile_picked_yhbays_mean_p_kernel(tc, x_words, x_scales, w1, offs, out):
             cols = slice(h * S // 1, (h + 1) * S // 1)
             nc.vector.tensor_copy(g_scales[:, cols], scales[:].indirect(offsets[:, h * S // 1 // 16 : (h + 1) * S // 1 // 16]))
             for q in range(4):
-                nc.sync.dma_start(plane[32 * q : 32 * q + 4, cols].bitcast(I32), g_scales[32 * q : 32 * q + 32 : 8, cols].bitcast(I32))
+                nc.sync.dma_start(plane[32 * q : 32 * q + 4, cols].bitcast(I32), g_scales[112 + 4 * q : 116 + 4 * q, cols].bitcast(I32))
 
         nc.vector.quantize_mx(out=w_codes[:].bitcast(FP8X4), scales=w_scales[:], in_=w_bf[:].rearrange("p m j -> p (m j)"))
 

@@ -17,119 +17,162 @@ ACT = mybir.ActivationFunctionType
 AXIS_X = mybir.AxisListType.X
 
 P = 128
+PACK = 4
+LIST_ROWS = 16
+SCALE_ROWS = K // 32
+QUADRANTS = 4
+QUADRANT_ROWS = SCALE_ROWS // QUADRANTS
+SCALE_BASE = P - SCALE_ROWS
+
 HALVES = 2
-HS = S // HALVES
-HV = HS // D
-HW = HV // D
+HALF_ENTRIES = S // HALVES
+HALF_DISTRICTS = HALF_ENTRIES // D
+HALF_STATES = HALF_DISTRICTS // D
 BANKS = 2
-BS = HS // BANKS
-BV = HV // BANKS
+BANK_ENTRIES = HALF_ENTRIES // BANKS
+BANK_DISTRICTS = HALF_DISTRICTS // BANKS
 LAG = 2
+
+VT_FLOOR = 0.05
+U_FLOOR = 0.25 * 0.1
 
 
 def tile_picked_yhbays_mean_p_kernel(tc, x_words, x_scales, w1, offs, out):
     nc = tc.nc
     with ExitStack() as ctx:
         sb = ctx.enter_context(tc.tile_pool(name="sb", bufs=1))
-        shared = ctx.enter_context(tc.tile_pool(name="shared", bufs=1))
+        reused = ctx.enter_context(tc.tile_pool(name="reused", bufs=1))
         ps = ctx.enter_context(tc.psum_pool(name="ps", bufs=1))
 
-        offsets = sb.tile([P, S // 16], U16, name="offsets")
+        offsets = sb.tile([P, S // LIST_ROWS], U16, name="offsets")
         words = sb.tile([P, T], U32, name="words", align_bytes=64)
-        scales = shared.tile([P, T], U8, name="scales", align_bytes=64, offset=0)
-        w_raw = sb.tile([P, 4, M], F32, name="w_raw", align_bytes=64)
+        scales = reused.tile([P, T], U8, name="scales", align_bytes=64, offset=0)
+        w_raw = sb.tile([P, PACK, M], F32, name="w_raw", align_bytes=64)
 
-        nc.vector.memset(scales[0:112, :].bitcast(I32), 0)
-        nc.sync.dma_start(scales[112:P, :].bitcast(I32), x_scales[0].bitcast(I32))
+        nc.vector.memset(scales[0:SCALE_BASE, :].bitcast(I32), 0)
+        nc.sync.dma_start(scales[SCALE_BASE:P, :].bitcast(I32), x_scales[0].bitcast(I32))
         nc.sync.dma_start(offsets[:], offs)
-        nc.scalar.dma_start(w_raw[:], w1.rearrange("(p j) m -> p j m", j=4))
-        nc.scalar.dma_start(words[:].bitcast(I32), x_words[0].rearrange("p n t -> p (n t)").bitcast(I32), max_dma_last_dim=4096)
+        nc.scalar.dma_start(w_raw[:], w1.rearrange("(p t) m -> p t m", t=PACK))
+        nc.scalar.dma_start(words[:].bitcast(I32), x_words[0].rearrange("p n t -> p (n t)").bitcast(I32))
 
         one = sb.tile([P, 1], F32, name="one")
         nc.vector.memset(one[:], 1.0)
         warm = sb.tile([P, 1], F32, name="warm")
         nc.scalar.activation(warm[:], one[:], ACT.Abs_reciprocal_sqrt)
 
-        w_bf = shared.tile([P, M, 4], BF16, name="w_bf", align_bytes=64, offset=T)
-        nc.scalar.copy(w_bf[:], w_raw[:].rearrange("p j m -> p m j"))
+        w_bf = reused.tile([P, M, PACK], BF16, name="w_bf", align_bytes=64, offset=T)
+        nc.scalar.copy(w_bf[:], w_raw[:].rearrange("p t m -> p m t"))
         w_codes = sb.tile([P, M], U32, name="w_codes", align_bytes=64)
         w_scales = sb.tile([P, M], U8, name="w_scales", align_bytes=64)
 
-        g_scales = sb.tile([P, S], U8, name="g_scales", align_bytes=64)
-        plane = sb.tile([P, S], U8, name="plane", align_bytes=64)
-        nc.vector.memset(plane[:].bitcast(I32), 0)
-        for h in range(1):
-            cols = slice(h * S // 1, (h + 1) * S // 1)
-            nc.vector.tensor_copy(g_scales[:, cols], scales[:].indirect(offsets[:, h * S // 1 // 16 : (h + 1) * S // 1 // 16]))
-            for q in range(4):
-                nc.sync.dma_start(plane[32 * q : 32 * q + 4, cols].bitcast(I32), g_scales[112 + 4 * q : 116 + 4 * q, cols].bitcast(I32))
+        picked_scales = sb.tile([P, S], U8, name="picked_scales", align_bytes=64)
+        placed_scales = sb.tile([P, S], U8, name="placed_scales", align_bytes=64)
+        nc.vector.memset(placed_scales[:].bitcast(I32), 0)
+        nc.vector.tensor_copy(picked_scales[:], scales[:].indirect(offsets[:]))
+        for q in range(QUADRANTS):
+            row = SCALE_BASE + QUADRANT_ROWS * q
+            nc.scalar.dma_start(
+                placed_scales[32 * q : 32 * q + QUADRANT_ROWS, :].bitcast(I32),
+                picked_scales[row : row + QUADRANT_ROWS, :].bitcast(I32),
+            )
 
-        nc.vector.quantize_mx(out=w_codes[:].bitcast(FP8X4), scales=w_scales[:], in_=w_bf[:].rearrange("p m j -> p (m j)"))
+        nc.vector.quantize_mx(
+            out=w_codes[:].bitcast(FP8X4), scales=w_scales[:], in_=w_bf[:].rearrange("p m t -> p (m t)")
+        )
 
-        g_words = shared.tile([P, S], U32, name="g_words", align_bytes=64, offset=T // 4)
-        ys = {}
+        w_bf_end = T + 2 * M * PACK
+        picked_words = reused.tile([P, S], U32, name="picked_words", align_bytes=64, offset=w_bf_end - PACK * S)
+        members = {}
         for h in range(HALVES):
-            nc.vector.tensor_copy(g_words[:, h * HS : (h + 1) * HS], words[:].indirect(offsets[:, h * HS // 16 : (h + 1) * HS // 16]))
+            first_entry = h * HALF_ENTRIES
+            half_offsets = offsets[:, first_entry // LIST_ROWS : (first_entry + HALF_ENTRIES) // LIST_ROWS]
+            nc.vector.tensor_copy(
+                picked_words[:, first_entry : first_entry + HALF_ENTRIES], words[:].indirect(half_offsets)
+            )
             for b in range(BANKS):
-                cols = slice(h * HS + b * BS, h * HS + (b + 1) * BS)
-                y = ps.tile([P, BS], F32, name=f"y{h}{b}")
-                nc.tensor.matmul_mx(out=y[:], lhsT=w_codes[:].bitcast(FP8X4), lhsT_scale=w_scales[:],
-                                    rhs=g_words[:, cols].bitcast(FP8X4), rhs_scale=plane[:, cols],
-                                    start=True, stop=True)
-                ys[h, b] = y[:].rearrange("p (v d) -> p d v", d=D)
+                entries = slice(first_entry + b * BANK_ENTRIES, first_entry + (b + 1) * BANK_ENTRIES)
+                y = ps.tile([P, BANK_ENTRIES], F32, name=f"y{h}{b}")
+                nc.tensor.matmul_mx(
+                    out=y[:],
+                    lhsT=w_codes[:].bitcast(FP8X4),
+                    lhsT_scale=w_scales[:],
+                    rhs=picked_words[:, entries].bitcast(FP8X4),
+                    rhs_scale=placed_scales[:, entries],
+                    start=True,
+                    stop=True,
+                )
+                members[h, b] = y[:].rearrange("p (v i) -> p i v", i=D)
 
-        def steps(h):
+        def by_state(tile):
+            return tile[:].rearrange("p (w i) -> p w i", i=D)
+
+        def to_districts(tile):
+            return tile[:].unsqueeze(2).to_broadcast([P, HALF_STATES, D])
+
+        def steps_of(h):
             def f32(name, *shape):
                 return sb.tile([P, *shape], F32, name=f"{name}{h}", align_bytes=64)
 
-            def per_state(t):
-                return t[:].unsqueeze(2).to_broadcast([P, HW, D])
-
-            def by_state(t):
-                return t[:].rearrange("p (w d) -> p w d", d=D)
-
-            late = [f32(f"late{b}", 2, BV) for b in range(BANKS)]
-            psum2 = f32("psum2", 2, HV)
-            pdiff = f32("pdiff", 2, HV)
-            pdiff2 = f32("pdiff2", 2, HV)
-            dsum, cross, cross2, q1, dev, within, dev2, den, root, inv, ta, tb, numer, res = [
-                f32(n, HV) for n in "dsum cross cross2 q1 dev within dev2 den root inv ta tb numer res".split()]
-            ssum = f32("ssum", HW)
-            between = f32("between", HW)
-            tt, stt, act = nc.vector.tensor_tensor, nc.vector.scalar_tensor_tensor, nc.scalar.activation
-
             def bank(b):
-                return slice(b * BV, (b + 1) * BV)
+                return slice(b * BANK_DISTRICTS, (b + 1) * BANK_DISTRICTS)
 
-            work = []
+            tt, stt, act = nc.vector.tensor_tensor, nc.vector.scalar_tensor_tensor, nc.scalar.activation
+            cd = [f32(f"cd{b}", 2, BANK_DISTRICTS) for b in range(BANKS)]
+            pair_sum = f32("pair_sum", 2, HALF_DISTRICTS)
+            pair_diff = f32("pair_diff", 2, HALF_DISTRICTS)
+            pair_sq = f32("pair_sq", 2, HALF_DISTRICTS)
+            dsum = f32("dsum", HALF_DISTRICTS)
+            cross = f32("cross", HALF_DISTRICTS)
+            cross_sq = f32("cross_sq", HALF_DISTRICTS)
+            pairs_sq = f32("pairs_sq", HALF_DISTRICTS)
+            dev = f32("dev", HALF_DISTRICTS)
+            within = f32("within", HALF_DISTRICTS)
+            dev_sq = f32("dev_sq", HALF_DISTRICTS)
+            den = f32("den", HALF_DISTRICTS)
+            root = f32("root", HALF_DISTRICTS)
+            inv = f32("inv", HALF_DISTRICTS)
+            state_term = f32("state_term", HALF_DISTRICTS)
+            district_term = f32("district_term", HALF_DISTRICTS)
+            numer = f32("numer", HALF_DISTRICTS)
+            res = f32("res", HALF_DISTRICTS)
+            ssum = f32("ssum", HALF_STATES)
+            between = f32("between", HALF_STATES)
+
+            steps = []
             for b in range(BANKS):
-                work.append(lambda b=b: nc.scalar.copy(late[b][:], ys[h, b][:, 2:4, :]))
-                work.append(lambda b=b: tt(psum2[:, :, bank(b)], ys[h, b][:, 0:2, :], late[b][:], ALU.add))
-            work.append(lambda: tt(dsum[:], psum2[:, 0, :], psum2[:, 1, :], ALU.add))
+                steps.append(lambda b=b: nc.scalar.copy(cd[b][:], members[h, b][:, 2:4, :]))
+                steps.append(lambda b=b: tt(pair_sum[:, :, bank(b)], members[h, b][:, 0:2, :], cd[b][:], ALU.add))
+            steps.append(lambda: tt(dsum[:], pair_sum[:, 0, :], pair_sum[:, 1, :], ALU.add))
             for b in range(BANKS):
-                work.append(lambda b=b: tt(pdiff[:, :, bank(b)], ys[h, b][:, 0:2, :], late[b][:], ALU.subtract))
-            work.extend([
+                steps.append(
+                    lambda b=b: tt(pair_diff[:, :, bank(b)], members[h, b][:, 0:2, :], cd[b][:], ALU.subtract)
+                )
+            steps.extend([
                 lambda: nc.vector.tensor_reduce(ssum[:], by_state(dsum), AXIS_X, ALU.add),
-                lambda: tt(cross[:], psum2[:, 0, :], psum2[:, 1, :], ALU.subtract),
-                lambda: act(pdiff2[:], pdiff[:], ACT.Square, scale=0.125),
-                lambda: stt(by_state(dev), per_state(ssum), -0.25, by_state(dsum), ALU.mult, ALU.add),
-                lambda: act(dev2[:], dev[:], ACT.Square, scale=0.125),
-                lambda: act(cross2[:], cross[:], ACT.Square, scale=0.125),
-                lambda: tt(q1[:], pdiff2[:, 0, :], pdiff2[:, 1, :], ALU.add),
-                lambda: nc.vector.tensor_reduce(between[:], by_state(dev2), AXIS_X, ALU.add),
-                lambda: stt(within[:], q1[:], 2.0, cross2[:], ALU.mult, ALU.add),
-                lambda: stt(by_state(den), per_state(between), 0.075, by_state(within), ALU.add, ALU.add),
+                lambda: tt(cross[:], pair_sum[:, 0, :], pair_sum[:, 1, :], ALU.subtract),
+                lambda: act(pair_sq[:], pair_diff[:], ACT.Square, scale=1 / 8),
+                lambda: stt(by_state(dev), to_districts(ssum), -1 / 4, by_state(dsum), ALU.mult, ALU.add),
+                lambda: act(dev_sq[:], dev[:], ACT.Square, scale=1 / 8),
+                lambda: act(cross_sq[:], cross[:], ACT.Square, scale=1 / 8),
+                lambda: tt(pairs_sq[:], pair_sq[:, 0, :], pair_sq[:, 1, :], ALU.add),
+                lambda: nc.vector.tensor_reduce(between[:], by_state(dev_sq), AXIS_X, ALU.add),
+                lambda: stt(within[:], pairs_sq[:], 2.0, cross_sq[:], ALU.mult, ALU.add),
+                lambda: stt(
+                    by_state(den), to_districts(between), VT_FLOOR + U_FLOOR, by_state(within), ALU.add, ALU.add
+                ),
                 lambda: act(root[:], den[:], ACT.Abs_reciprocal_sqrt),
-                lambda: stt(by_state(ta), by_state(within), 0.025, per_state(ssum), ALU.add, ALU.mult),
-                lambda: stt(by_state(tb), per_state(between), 0.05, by_state(dsum), ALU.add, ALU.mult),
-                lambda: act(inv[:], root[:], ACT.Square, scale=0.25),
-                lambda: stt(numer[:], tb[:], 4.0, ta[:], ALU.mult, ALU.add),
+                lambda: stt(by_state(state_term), by_state(within), U_FLOOR, to_districts(ssum), ALU.add, ALU.mult),
+                lambda: stt(
+                    by_state(district_term), to_districts(between), VT_FLOOR, by_state(dsum), ALU.add, ALU.mult
+                ),
+                lambda: act(inv[:], root[:], ACT.Square, scale=1 / 4),
+                lambda: stt(numer[:], district_term[:], 4.0, state_term[:], ALU.mult, ALU.add),
                 lambda: tt(res[:], numer[:], inv[:], ALU.mult),
-                lambda: nc.sync.dma_start(out[:, h * HV : (h + 1) * HV], res[:]),
+                lambda: nc.sync.dma_start(out[:, h * HALF_DISTRICTS : (h + 1) * HALF_DISTRICTS], res[:]),
             ])
-            return work
+            return steps
 
-        first, second = steps(0), steps(1)
+        first, second = steps_of(0), steps_of(1)
         for i in range(len(first) + LAG):
             if i >= LAG:
                 second[i - LAG]()

from contextlib import ExitStack

import concourse.mybir as mybir

K, T, S, D, M = 512, 4096, 1024, 4, 128
FLOPS = 2 * K * M * S

F32 = mybir.dt.float32
BF16 = mybir.dt.bfloat16
I32 = mybir.dt.int32
U32 = mybir.dt.uint32
U16 = mybir.dt.uint16
U8 = mybir.dt.uint8
FP8X4 = mybir.dt.float8_e4m3fn_x4
ALU = mybir.AluOpType
ACT = mybir.ActivationFunctionType
AXIS_X = mybir.AxisListType.X

P = 128
PACK = 4
LIST_ROWS = 16
SCALE_ROWS = K // 32
QUADRANTS = 4
QUADRANT_ROWS = SCALE_ROWS // QUADRANTS
SCALE_BASE = P - SCALE_ROWS

HALVES = 2
HALF_ENTRIES = S // HALVES
HALF_DISTRICTS = HALF_ENTRIES // D
HALF_STATES = HALF_DISTRICTS // D
BANKS = 2
BANK_ENTRIES = HALF_ENTRIES // BANKS
BANK_DISTRICTS = HALF_DISTRICTS // BANKS
LAG = 2

VT_FLOOR = 0.05
U_FLOOR = 0.25 * 0.1


def tile_picked_yhbays_mean_p_kernel(tc, x_words, x_scales, w1, offs, out):
    nc = tc.nc
    with ExitStack() as ctx:
        sb = ctx.enter_context(tc.tile_pool(name="sb", bufs=1))
        reused = ctx.enter_context(tc.tile_pool(name="reused", bufs=1))
        ps = ctx.enter_context(tc.psum_pool(name="ps", bufs=1))

        offsets = sb.tile([P, S // LIST_ROWS], U16, name="offsets")
        words = sb.tile([P, T], U32, name="words", align_bytes=64)
        scales = reused.tile([P, T], U8, name="scales", align_bytes=64, offset=0)
        w_raw = sb.tile([P, PACK, M], F32, name="w_raw", align_bytes=64)

        nc.vector.memset(scales[0:SCALE_BASE, :].bitcast(I32), 0)
        nc.sync.dma_start(scales[SCALE_BASE:P, :].bitcast(I32), x_scales[0].bitcast(I32))
        nc.sync.dma_start(offsets[:], offs)
        nc.scalar.dma_start(w_raw[:], w1.rearrange("(p t) m -> p t m", t=PACK))
        nc.scalar.dma_start(words[:].bitcast(I32), x_words[0].rearrange("p n t -> p (n t)").bitcast(I32))

        one = sb.tile([P, 1], F32, name="one")
        nc.vector.memset(one[:], 1.0)
        warm = sb.tile([P, 1], F32, name="warm")
        nc.scalar.activation(warm[:], one[:], ACT.Abs_reciprocal_sqrt)

        w_bf = reused.tile([P, M, PACK], BF16, name="w_bf", align_bytes=64, offset=T)
        nc.scalar.copy(w_bf[:], w_raw[:].rearrange("p t m -> p m t"))
        w_codes = sb.tile([P, M], U32, name="w_codes", align_bytes=64)
        w_scales = sb.tile([P, M], U8, name="w_scales", align_bytes=64)

        picked_scales = sb.tile([P, S], U8, name="picked_scales", align_bytes=64)
        placed_scales = sb.tile([P, S], U8, name="placed_scales", align_bytes=64)
        nc.vector.memset(placed_scales[:].bitcast(I32), 0)
        nc.vector.tensor_copy(picked_scales[:], scales[:].indirect(offsets[:]))
        for q in range(QUADRANTS):
            row = SCALE_BASE + QUADRANT_ROWS * q
            nc.scalar.dma_start(
                placed_scales[32 * q : 32 * q + QUADRANT_ROWS, :].bitcast(I32),
                picked_scales[row : row + QUADRANT_ROWS, :].bitcast(I32),
            )

        nc.vector.quantize_mx(
            out=w_codes[:].bitcast(FP8X4), scales=w_scales[:], in_=w_bf[:].rearrange("p m t -> p (m t)")
        )

        w_bf_end = T + 2 * M * PACK
        picked_words = reused.tile([P, S], U32, name="picked_words", align_bytes=64, offset=w_bf_end - PACK * S)
        members = {}
        for h in range(HALVES):
            first_entry = h * HALF_ENTRIES
            half_offsets = offsets[:, first_entry // LIST_ROWS : (first_entry + HALF_ENTRIES) // LIST_ROWS]
            nc.vector.tensor_copy(
                picked_words[:, first_entry : first_entry + HALF_ENTRIES], words[:].indirect(half_offsets)
            )
            for b in range(BANKS):
                entries = slice(first_entry + b * BANK_ENTRIES, first_entry + (b + 1) * BANK_ENTRIES)
                y = ps.tile([P, BANK_ENTRIES], F32, name=f"y{h}{b}")
                nc.tensor.matmul_mx(
                    out=y[:],
                    lhsT=w_codes[:].bitcast(FP8X4),
                    lhsT_scale=w_scales[:],
                    rhs=picked_words[:, entries].bitcast(FP8X4),
                    rhs_scale=placed_scales[:, entries],
                    start=True,
                    stop=True,
                )
                members[h, b] = y[:].rearrange("p (v i) -> p i v", i=D)

        def by_state(tile):
            return tile[:].rearrange("p (w i) -> p w i", i=D)

        def to_districts(tile):
            return tile[:].unsqueeze(2).to_broadcast([P, HALF_STATES, D])

        def steps_of(h):
            def f32(name, *shape):
                return sb.tile([P, *shape], F32, name=f"{name}{h}", align_bytes=64)

            def bank(b):
                return slice(b * BANK_DISTRICTS, (b + 1) * BANK_DISTRICTS)

            tt, stt, act = nc.vector.tensor_tensor, nc.vector.scalar_tensor_tensor, nc.scalar.activation
            cd = [f32(f"cd{b}", 2, BANK_DISTRICTS) for b in range(BANKS)]
            pair_sum = f32("pair_sum", 2, HALF_DISTRICTS)
            pair_diff = f32("pair_diff", 2, HALF_DISTRICTS)
            pair_sq = f32("pair_sq", 2, HALF_DISTRICTS)
            dsum = f32("dsum", HALF_DISTRICTS)
            cross = f32("cross", HALF_DISTRICTS)
            cross_sq = f32("cross_sq", HALF_DISTRICTS)
            pairs_sq = f32("pairs_sq", HALF_DISTRICTS)
            dev = f32("dev", HALF_DISTRICTS)
            within = f32("within", HALF_DISTRICTS)
            dev_sq = f32("dev_sq", HALF_DISTRICTS)
            den = f32("den", HALF_DISTRICTS)
            root = f32("root", HALF_DISTRICTS)
            inv = f32("inv", HALF_DISTRICTS)
            state_term = f32("state_term", HALF_DISTRICTS)
            district_term = f32("district_term", HALF_DISTRICTS)
            numer = f32("numer", HALF_DISTRICTS)
            res = f32("res", HALF_DISTRICTS)
            ssum = f32("ssum", HALF_STATES)
            between = f32("between", HALF_STATES)

            steps = []
            for b in range(BANKS):
                steps.append(lambda b=b: nc.scalar.copy(cd[b][:], members[h, b][:, 2:4, :]))
                steps.append(lambda b=b: tt(pair_sum[:, :, bank(b)], members[h, b][:, 0:2, :], cd[b][:], ALU.add))
            steps.append(lambda: tt(dsum[:], pair_sum[:, 0, :], pair_sum[:, 1, :], ALU.add))
            for b in range(BANKS):
                steps.append(
                    lambda b=b: tt(pair_diff[:, :, bank(b)], members[h, b][:, 0:2, :], cd[b][:], ALU.subtract)
                )
            steps.extend([
                lambda: nc.vector.tensor_reduce(ssum[:], by_state(dsum), AXIS_X, ALU.add),
                lambda: tt(cross[:], pair_sum[:, 0, :], pair_sum[:, 1, :], ALU.subtract),
                lambda: act(pair_sq[:], pair_diff[:], ACT.Square, scale=1 / 8),
                lambda: stt(by_state(dev), to_districts(ssum), -1 / 4, by_state(dsum), ALU.mult, ALU.add),
                lambda: act(dev_sq[:], dev[:], ACT.Square, scale=1 / 8),
                lambda: act(cross_sq[:], cross[:], ACT.Square, scale=1 / 8),
                lambda: tt(pairs_sq[:], pair_sq[:, 0, :], pair_sq[:, 1, :], ALU.add),
                lambda: nc.vector.tensor_reduce(between[:], by_state(dev_sq), AXIS_X, ALU.add),
                lambda: stt(within[:], pairs_sq[:], 2.0, cross_sq[:], ALU.mult, ALU.add),
                lambda: stt(
                    by_state(den), to_districts(between), VT_FLOOR + U_FLOOR, by_state(within), ALU.add, ALU.add
                ),
                lambda: act(root[:], den[:], ACT.Abs_reciprocal_sqrt),
                lambda: stt(by_state(state_term), by_state(within), U_FLOOR, to_districts(ssum), ALU.add, ALU.mult),
                lambda: stt(
                    by_state(district_term), to_districts(between), VT_FLOOR, by_state(dsum), ALU.add, ALU.mult
                ),
                lambda: act(inv[:], root[:], ACT.Square, scale=1 / 4),
                lambda: stt(numer[:], district_term[:], 4.0, state_term[:], ALU.mult, ALU.add),
                lambda: tt(res[:], numer[:], inv[:], ALU.mult),
                lambda: nc.sync.dma_start(out[:, h * HALF_DISTRICTS : (h + 1) * HALF_DISTRICTS], res[:]),
            ])
            return steps

        first, second = steps_of(0), steps_of(1)
        for i in range(len(first) + LAG):
            if i >= LAG:
                second[i - LAG]()
            if i < len(first):
                first[i]()
